import numpy as np
import ml_dtypes


def mxq(x, axis, fmt="e4m3"):
    dtype, down = {"e4m3": (ml_dtypes.float8_e4m3fn, 7), "e5m2": (ml_dtypes.float8_e5m2, 14)}[fmt]
    v = np.moveaxis(np.asarray(x, np.float32).astype(ml_dtypes.bfloat16).astype(np.float64), axis, -1)
    blocks = v.reshape(v.shape[:-1] + (-1, 32))
    amax = np.abs(blocks).max(-1, keepdims=True)
    byte = np.maximum(np.where(amax > 0, np.frexp(amax)[1] - 1 + 127, 0) - down, 1)
    scale = np.exp2(byte - 127.0)
    codes = (blocks / scale).astype(np.float32).astype(dtype).astype(np.float64)
    return np.moveaxis((codes * scale).reshape(v.shape), -1, axis)


WIDE = False


def mx_kscale(k):
    if not WIDE:
        return np.ones(k)
    levels = np.array([10, -10, 5, -5, 0])
    if k % 512:
        return np.exp2(np.random.permutation(np.resize(levels, k // 32))).repeat(32)
    a = np.empty((k // 512, 16))
    for p in range(k // 512):
        a[p, :8] = np.random.permutation(np.resize(levels, 8))
        for g in range(8):
            far = levels[np.abs(levels - a[p, g]) >= 10]
            a[p, g + 8] = far[np.random.randint(len(far))]
    return np.exp2(a.ravel()).repeat(32)


def f64(x):
    return np.asarray(x).astype(np.float64)


def striped(idx):
    return np.tile(idx.reshape(-1, 16).T, (8, 1)).astype(np.uint16)


def unstriped(offs):
    return offs[:16].T.reshape(-1).astype(np.int64)


def striped8(idx):
    return np.concatenate([x.reshape(-1, 16).T for x in idx]).astype(np.uint16)


def runs(offs, k):
    lists = np.stack([offs[16 * r : 16 * r + 16].T.reshape(-1) for r in range(8)]).astype(np.int64)
    return lists[np.arange(k) % 512 // 64]


def pack_weight(w):
    k, n = w.shape
    w = f64(np.asarray(w, np.float32).astype(ml_dtypes.bfloat16)).reshape(k // 32, 32, n)
    amax = np.abs(w).max(1)
    byte = np.clip(np.where(amax > 0, np.frexp(amax)[1] - 1 + 127 - 7, 1), 1, 254)
    scaled = (w * np.exp2(127.0 - byte)[:, None, :]).reshape(k, n).astype(np.float32)
    words = np.ascontiguousarray(scaled.reshape(k // 512, 128, 4, n).transpose(0, 1, 3, 2)).astype(ml_dtypes.float8_e4m3fn).view(np.uint8)
    return words, np.ascontiguousarray(byte.astype(np.uint8).reshape(k // 512, 16, n))


def unpack_weight(words, scales):
    g, p, n, _ = words.shape
    vals = np.ascontiguousarray(words).view(ml_dtypes.float8_e4m3fn).astype(np.float64) * np.repeat(np.exp2(scales.astype(np.float64) - 127.0), 8, axis=1)[..., None]
    return vals.transpose(0, 1, 3, 2).reshape(g * 512, n)


def sigmoid(v):
    return 1.0 / (1.0 + np.exp(-np.maximum(v, -700.0)))


K, T, S, V, N, H = 512, 2048, 512, 256, 512, 512


def setup_inputs():
    n = np.random.standard_normal
    s = mx_kscale(K)[:, None]
    u = mx_kscale(H)
    packed_xT = pack_weight(n((K, T)) * s)
    return {
        "x_words": packed_xT[0],
        "x_scales": packed_xT[1],
        "w1": (n((K, H)) / np.sqrt(K) / s).astype(np.float32),
        "gn": (np.random.uniform(0.5, 1.5, (H, 1)) * u[:, None]).astype(np.float32),
        "w2": (n((H, N)) / np.sqrt(2 * H) / u[:, None]).astype(np.float32),
        "w3": (n((K, N)) / np.sqrt(2 * K) / s).astype(np.float32),
        "offs": striped(np.random.permutation(T)[:S]),
        "n1": striped(np.random.permutation(S)),
        "hz": striped8(np.random.randint(0, T, (8, V))),
        "n2": striped8(np.stack([np.random.permutation(V) for _ in range(8)])),
        "n3": striped8(np.stack([np.random.permutation(V) for _ in range(8)])),
    }


def reference(x_words, x_scales, w1, gn, w2, w3, offs, n1, hz, n2, n3):
    xq = unpack_weight(x_words, x_scales)[:, unstriped(offs)]
    y = mxq(f64(w1), 0, "e4m3").T @ xq
    ln = y[:, unstriped(n1)]
    mx = ln.reshape(H, V, 2).max(axis=2)
    mn = ln.reshape(H, V, 2).min(axis=2)
    z = f64(gn) * (mx * sigmoid(mn))
    x_hz = unpack_weight(x_words, x_scales)[np.arange(K)[:, None], runs(hz, K)]
    h = mxq(f64(w2), 0, "e4m3").T @ mxq(z, 0, "e4m3") + mxq(f64(w3), 0, "e4m3").T @ x_hz
    return (np.tanh(h[np.arange(N)[:, None], runs(n2, N)] - h)) * (h[np.arange(N)[:, None], runs(n3, N)])

@@ -1,0 +1,269 @@
+from contextlib import ExitStack
+
+import concourse.mybir as mybir
+
+K, T, S, V, N, H = 512, 2048, 512, 256, 512, 512
+FLOPS = 2 * K * H * S + 2 * H * N * V + 2 * K * N * V
+
+F32 = mybir.dt.float32
+BF16 = mybir.dt.bfloat16
+I32 = mybir.dt.int32
+U32 = mybir.dt.uint32
+U16 = mybir.dt.uint16
+U8 = mybir.dt.uint8
+FP8X4 = mybir.dt.float8_e4m3fn_x4
+ALU = mybir.AluOpType
+ACT = mybir.ActivationFunctionType
+
+P = 128
+PACK = 4
+HALF = V // 2
+
+
+def tile_picked_mixhhpgatefdif_none_p_kernel(tc, x_words, x_scales, w1, gn, w2, w3, offs, n1, hz, n2, n3, out):
+    nc = tc.nc
+    with ExitStack() as ctx:
+        lists = ctx.enter_context(tc.tile_pool(name="lists", bufs=1))
+        keep = ctx.enter_context(tc.tile_pool(name="keep", bufs=1))
+        psum = ctx.enter_context(tc.psum_pool(name="psum", bufs=1))
+
+        def load_list(src, name):
+            held = lists.tile(list(src.shape), U16, name=name)
+            nc.sync.dma_start(out=held[:], in_=src)
+            return held
+
+        x_sc = keep.tile([P, T], U8, name="x_sc", align_bytes=64)
+        nc.gpsimd.memset(x_sc[:].bitcast(I32), 0)
+        w1_raw = keep.tile([P, PACK, H], F32, name="w1_raw")
+        nc.sync.dma_start(out=w1_raw[:], in_=w1.rearrange("(p j) c -> p j c", j=PACK))
+        x_sc32 = x_sc[:].bitcast(I32)
+        rows32 = x_scales[0].bitcast(I32)
+        for r in range(4):
+            if r < 2:
+                nc.sync.dma_start(out=x_sc32[r:P:32, :], in_=rows32[r:16:4, :])
+            else:
+                nc.sync.dma_start(
+                    out=x_sc32[r:P:16, :],
+                    in_=rows32[r:16:4, :].unsqueeze(1).to_broadcast([4, 2, T // 4]),
+                )
+        offs_sb = load_list(offs, "offs_sb")
+        hz_sb = load_list(hz, "hz_sb")
+        x_wd = keep.tile([P, T], U32, name="x_wd", align_bytes=64)
+        nc.sync.dma_start(out=x_wd[:].bitcast(I32), in_=x_words[0].rearrange("p n t -> p (n t)").bitcast(I32))
+        n1_sb = load_list(n1, "n1_sb")
+        gains = []
+        gn_rows = gn.rearrange("(q t r) o -> t q r o", t=PACK, r=8)
+        for t in range(PACK):
+            gain = keep.tile([P, 1], F32, name=f"gain{t}")
+            with nc.allow_non_contiguous_dma(reason="one gain a partition"):
+                nc.gpsimd.dma_start(out=gain[:], in_=gn_rows[t])
+            gains.append(gain)
+        w2_raw = keep.tile([P, PACK, N], F32, name="w2_raw")
+        w2_rows = w2.rearrange("(q t r) c -> t q r c", t=PACK, r=8)
+        for t in range(PACK):
+            nc.sync.dma_start(out=w2_raw[:, t, :], in_=w2_rows[t])
+        w3_raw = keep.tile([P, PACK, N], F32, name="w3_raw")
+        nc.sync.dma_start(out=w3_raw[:], in_=w3.rearrange("(p j) c -> p j c", j=PACK))
+        n2_sb = load_list(n2, "n2_sb")
+        n3_sb = load_list(n3, "n3_sb")
+
+        def deal(copy, dst, raw, t):
+            copy(
+                out=dst.rearrange("p (q a i) j -> p q a j i", a=2, i=4),
+                in_=raw.rearrange("p j (q t a i) -> p t q a j i", t=PACK, a=2, i=4)[:, t],
+            )
+
+        def quantise(grouped, width, name):
+            codes = keep.tile([P, width], U32, name=name + "_codes", align_bytes=64)
+            scales = keep.tile([P, width], U8, name=name + "_scales", align_bytes=64)
+            nc.vector.quantize_mx(out=codes[:].bitcast(FP8X4), scales=scales[:], in_=grouped.rearrange("p c j -> p (c j)"))
+            return codes, scales
+
+        def product(acc, weights, moving, start, stop):
+            nc.tensor.matmul_mx(
+                out=acc,
+                lhsT=weights[0][:].bitcast(FP8X4),
+                lhsT_scale=weights[1][:],
+                rhs=moving[0][:].bitcast(FP8X4),
+                rhs_scale=moving[1][:],
+                start=start,
+                stop=stop,
+            )
+
+        def rounded(copy, raw, t, name, dst=None):
+            if dst is None:
+                dst = keep.tile([P, P, PACK], BF16, name=name + "_bf", align_bytes=64)[:]
+            deal(copy, dst, raw[:], t)
+            return dst
+
+        w1_bf = [rounded(nc.scalar.copy, w1_raw, t, f"w1_{t}") for t in range(PACK)]
+
+        xq_sc = keep.tile([P, S], U8, name="xq_sc", align_bytes=64)
+        nc.vector.tensor_copy(out=xq_sc[:], in_=x_sc[:].indirect(offs_sb[:]))
+        xh_raw = keep.tile([P, V], U8, name="xh_raw", align_bytes=64)
+        nc.vector.tensor_copy(out=xh_raw[:], in_=x_sc[:].indirect(hz_sb[:]))
+        xh_sc = keep.tile([P, V], U8, name="xh_sc", align_bytes=64)
+        nc.vector.tensor_copy(out=xh_sc[:].bitcast(I32), in_=xh_raw[:].bitcast(I32))
+        for r in (2, 3):
+            nc.sync.dma_start(out=xh_sc[:].bitcast(I32)[r:P:32, :], in_=xh_raw[:].bitcast(I32)[16 + r : P : 32, :])
+        w1_q = [quantise(w1_bf[t], P, f"w1_{t}") for t in range(PACK - 1)]
+        xq_wd = keep.tile([P, S], U32, name="xq_wd", align_bytes=64)
+        rows = [keep.tile([P, S], F32, name=f"rows{t}") for t in range(PACK)]
+        y0_ps = [psum.tile([P, S // 2], F32, name=f"y0_ps{u}", tag=f"y0_ps{u}") for u in range(2)]
+        y_ps = {t: psum.tile([P, S], F32, name=f"y_ps{t}") for t in range(1, PACK)}
+        for u in range(2):
+            cols = slice(u * (S // 2), (u + 1) * (S // 2))
+            nc.vector.tensor_copy(out=xq_wd[:, cols], in_=x_wd[:].indirect(offs_sb[:, u * 16 : (u + 1) * 16]))
+            product(y0_ps[u][:], w1_q[0], (xq_wd[:, cols], xq_sc[:, cols]), True, True)
+            product(y_ps[1][:, cols], w1_q[1], (xq_wd[:, cols], xq_sc[:, cols]), True, True)
+            nc.scalar.copy(out=rows[0][:, cols], in_=y0_ps[u][:])
+        w1_q.append(quantise(w1_bf[3], P, "w1_3"))
+        for t in range(2, PACK):
+            product(y_ps[t][:], w1_q[t], (xq_wd, xq_sc), True, True)
+        xh_wd = keep.tile([P, V], U32, name="xh_wd", align_bytes=64)
+        nc.vector.tensor_copy(out=xh_wd[:], in_=x_wd[:].indirect(hz_sb[:]))
+
+        big = keep.tile([P, PACK, V], F32, name="big")
+        gained = keep.tile([P, PACK, V], F32, name="gained", tag="later", align_bytes=64)
+        gate = keep.tile([P, PACK, V], F32, name="gate")
+        small = keep.tile([P, PACK, V], F32, name="small", tag="late", align_bytes=64)
+        z_bf = keep.tile([P, V, PACK], BF16, name="z_bf", align_bytes=64)
+        z_wd = keep.tile([P, V], U32, name="z_wd", align_bytes=64)
+        z_sc = keep.tile([P, V], U8, name="z_sc", align_bytes=64)
+
+        def line_up(lined, t, v0, v1):
+            nc.scalar.activation(
+                out=lined.rearrange("p v e -> p (v e)"),
+                in_=rows[t][:].indirect(n1_sb[:, v0 // 8 : v1 // 8]),
+                func=ACT.Copy,
+            )
+
+        def smaller(low, lined):
+            nc.vector.tensor_tensor(out=low, in0=lined[:, :, :, 0], in1=lined[:, :, :, 1], op=ALU.min)
+
+        def larger(high, lined):
+            nc.vector.tensor_tensor(out=high, in0=lined[:, :, :, 0], in1=lined[:, :, :, 1], op=ALU.max)
+
+        def gate_of(dst, low):
+            nc.scalar.activation(out=dst, in_=low, func=ACT.Sigmoid)
+
+        def gain_on(t, v0, v1):
+            nc.vector.tensor_scalar(out=gained[:, t, v0:v1], in0=big[:, t, v0:v1], scalar1=gains[t][:], scalar2=None, op0=ALU.mult)
+
+        def make_z(v0, v1):
+            nc.vector.tensor_tensor(
+                out=z_bf[:, v0:v1, :].rearrange("p (c i) t -> p c t i", i=4),
+                in0=gained[:, :, v0:v1].rearrange("p t (c i) -> p c t i", i=4),
+                in1=gate[:, :, v0:v1].rearrange("p t (c i) -> p c t i", i=4),
+                op=ALU.mult,
+            )
+
+        def quantise_z(v0, v1):
+            nc.vector.quantize_mx(out=z_wd[:, v0:v1].bitcast(FP8X4), scales=z_sc[:, v0:v1], in_=z_bf[:, v0:v1, :].rearrange("p c j -> p (c j)"))
+
+        w2_q, w3_q = {}, {}
+        Q = V // 4
+        for t in range(1, PACK):
+            nc.vector.tensor_copy(out=rows[t][:], in_=y_ps[t][:])
+        lined = keep.tile([P, PACK, V, 2], F32, name="lined")
+
+        def extremes(t, v0, v1):
+            line_up(lined[:, t, v0:v1], t, v0, v1) if v1 - v0 == HALF else [line_up(lined[:, t, a : a + HALF], t, a, a + HALF) for a in (0, HALF)]
+            smaller(small[:, t : t + 1, v0:v1], lined[:, t : t + 1, v0:v1])
+            larger(big[:, t : t + 1, v0:v1], lined[:, t : t + 1, v0:v1])
+
+        extremes(0, 0, V)
+        w2_bf0 = rounded(nc.vector.tensor_copy, w2_raw, 0, "w2_0")
+        gain_on(0, 0, V)
+        extremes(1, 0, V)
+        w2_q[0] = quantise(w2_bf0, P, "w2_0")
+        gain_on(1, 0, V)
+        w3_bf0 = rounded(nc.vector.tensor_copy, w3_raw, 0, "w3_0")
+        extremes(2, 0, V)
+        extremes(3, 0, HALF)
+        gain_on(2, 0, V)
+        w3_q[0] = quantise(w3_bf0, P, "w3_0")
+        gain_on(3, 0, HALF)
+        extremes(3, HALF, V)
+        for u in range(4):
+            gate_of(gate[:, :, u * Q : (u + 1) * Q], small[:, :, u * Q : (u + 1) * Q])
+        make_z(0, Q)
+        gain_on(3, HALF, V)
+        make_z(Q, HALF)
+        make_z(HALF, 3 * Q)
+        quantise_z(0, HALF)
+        make_z(3 * Q, V)
+        quantise_z(HALF, 3 * Q)
+        quantise_z(3 * Q, V)
+        later = keep.tile([P, 3, P, PACK], BF16, name="later_bf", tag="later", align_bytes=64)
+        late = keep.tile([P, 3, P, PACK], BF16, name="late_bf", tag="late", align_bytes=64)
+
+        out_rows = out.rearrange("(q t r) v -> t q r v", t=PACK, r=8)
+        h_ps = [psum.tile([P, V], F32, name=f"h_ps{t}", tag="y0_ps0" if t == 3 else f"h_ps{t}") for t in range(PACK)]
+
+        def make_h(t):
+            product(h_ps[t][:], w2_q[t], (z_wd, z_sc), True, False)
+            product(h_ps[t][:], w3_q[t], (xh_wd, xh_sc), False, True)
+
+        def make_first_h():
+            product(h_ps[0][:], w3_q[0], (xh_wd, xh_sc), True, False)
+            for u in range(2):
+                cols = slice(u * HALF, (u + 1) * HALF)
+                product(h_ps[0][:, cols], w2_q[0], (z_wd[:, cols], z_sc[:, cols]), False, u == 1)
+
+        def fetch_h(t):
+            nc.vector.tensor_copy(out=rows[t][:, :V], in_=h_ps[t][:])
+
+        ahead = [keep.tile([P, V], F32, name=f"ahead{t}") for t in range(PACK)]
+        factor = [keep.tile([P, V], F32, name=f"factor{t}") for t in range(PACK)]
+        diff = [keep.tile([P, V], F32, name=f"diff{t}") for t in range(PACK)]
+        bent = [keep.tile([P, V], F32, name=f"bent{t}") for t in range(PACK)]
+
+        def fetch(dst, t, offsets):
+            nc.scalar.activation(out=dst[:], in_=rows[t][:].indirect(offsets[:]), func=ACT.Copy)
+
+        def look_up(t):
+            fetch(ahead[t], t, n2_sb)
+            fetch(factor[t], t, n3_sb)
+
+        def bend(t):
+            nc.vector.tensor_tensor(out=diff[t][:], in0=ahead[t][:], in1=h_ps[t][:], op=ALU.subtract)
+            nc.scalar.activation(out=bent[t][:], in_=diff[t][:], func=ACT.Tanh)
+
+        def finish(t):
+            result = keep.tile([P, V], F32, name=f"result{t}")
+            nc.vector.tensor_tensor(out=result[:], in0=bent[t][:], in1=factor[t][:], op=ALU.mult)
+            nc.sync.dma_start(out=out_rows[t], in_=result[:])
+
+        make_first_h()
+        fetch_h(0)
+        look_up(0)
+        rounded(nc.scalar.copy, w2_raw, 1, "w2_1", late[:, 0])
+        rounded(nc.scalar.copy, w3_raw, 1, "w3_1", late[:, 1])
+        rounded(nc.scalar.copy, w3_raw, 2, "w3_2", late[:, 2])
+        rounded(nc.vector.tensor_copy, w2_raw, 2, "w2_2", later[:, 0])
+        w2_q[1] = quantise(late[:, 0], P, "w2_1")
+        w3_q[1] = quantise(late[:, 1], P, "w3_1")
+        make_h(1)
+        w2_q[2] = quantise(later[:, 0], P, "w2_2")
+        w3_q[2] = quantise(late[:, 2], P, "w3_2")
+        make_h(2)
+        fetch_h(1)
+        look_up(1)
+        rounded(nc.vector.tensor_copy, w2_raw, 3, "w2_3", later[:, 1])
+        rounded(nc.vector.tensor_copy, w3_raw, 3, "w3_3", later[:, 2])
+        bend(0)
+        w2_q[3] = quantise(later[:, 1], P, "w2_3")
+        w3_q[3] = quantise(later[:, 2], P, "w3_3")
+        make_h(3)
+        fetch_h(2)
+        look_up(2)
+        bend(1)
+        fetch_h(3)
+        look_up(3)
+        finish(0)
+        bend(2)
+        finish(1)
+        bend(3)
+        finish(2)
+        finish(3)

@@ -33,9 +33,18 @@ def tile_picked_mixhhpgatefdif_none_p_kernel(tc, x_words, x_scales, w1, gn, w2, 
             return held
 
         x_sc = keep.tile([P, T], U8, name="x_sc", align_bytes=64)
-        nc.gpsimd.memset(x_sc[:].bitcast(I32), 0)
+        nc.vector.memset(x_sc[:].bitcast(I32), 0)
+        gains = []
+        gn_rows = gn.rearrange("(q t r) o -> t q r o", t=PACK, r=8)
+        for t in range(PACK):
+            gain = keep.tile([P, 1], F32, name=f"gain{t}")
+            with nc.allow_non_contiguous_dma(reason="one gain a partition"):
+                nc.gpsimd.dma_start(out=gain[:], in_=gn_rows[t])
+            gains.append(gain)
+        offs_sb = load_list(offs, "offs_sb")
         w1_raw = keep.tile([P, PACK, H], F32, name="w1_raw")
-        nc.sync.dma_start(out=w1_raw[:], in_=w1.rearrange("(p j) c -> p j c", j=PACK))
+        w1_rows = w1.rearrange("(p j) c -> p j c", j=PACK)
+        nc.sync.dma_start(out=w1_raw[:, :2, :], in_=w1_rows[:, :2, :])
         x_sc32 = x_sc[:].bitcast(I32)
         rows32 = x_scales[0].bitcast(I32)
         for r in range(4):
@@ -46,26 +55,17 @@ def tile_picked_mixhhpgatefdif_none_p_kernel(tc, x_words, x_scales, w1, gn, w2, 
                     out=x_sc32[r:P:16, :],
                     in_=rows32[r:16:4, :].unsqueeze(1).to_broadcast([4, 2, T // 4]),
                 )
-        offs_sb = load_list(offs, "offs_sb")
         hz_sb = load_list(hz, "hz_sb")
+        nc.sync.dma_start(out=w1_raw[:, 2:, :], in_=w1_rows[:, 2:, :])
         x_wd = keep.tile([P, T], U32, name="x_wd", align_bytes=64)
         nc.sync.dma_start(out=x_wd[:].bitcast(I32), in_=x_words[0].rearrange("p n t -> p (n t)").bitcast(I32))
         n1_sb = load_list(n1, "n1_sb")
-        gains = []
-        gn_rows = gn.rearrange("(q t r) o -> t q r o", t=PACK, r=8)
-        for t in range(PACK):
-            gain = keep.tile([P, 1], F32, name=f"gain{t}")
-            with nc.allow_non_contiguous_dma(reason="one gain a partition"):
-                nc.gpsimd.dma_start(out=gain[:], in_=gn_rows[t])
-            gains.append(gain)
         w2_raw = keep.tile([P, PACK, N], F32, name="w2_raw")
         w2_rows = w2.rearrange("(q t r) c -> t q r c", t=PACK, r=8)
         for t in range(PACK):
             nc.sync.dma_start(out=w2_raw[:, t, :], in_=w2_rows[t])
         w3_raw = keep.tile([P, PACK, N], F32, name="w3_raw")
         nc.sync.dma_start(out=w3_raw[:], in_=w3.rearrange("(p j) c -> p j c", j=PACK))
-        n2_sb = load_list(n2, "n2_sb")
-        n3_sb = load_list(n3, "n3_sb")
 
         def deal(copy, dst, raw, t):
             copy(
@@ -96,7 +96,7 @@ def tile_picked_mixhhpgatefdif_none_p_kernel(tc, x_words, x_scales, w1, gn, w2, 
             deal(copy, dst, raw[:], t)
             return dst
 
-        w1_bf = [rounded(nc.scalar.copy, w1_raw, t, f"w1_{t}") for t in range(PACK)]
+        w1_bf = [rounded(nc.scalar.copy if t < 3 else nc.vector.tensor_copy, w1_raw, t, f"w1_{t}") for t in range(PACK)]
 
         xq_sc = keep.tile([P, S], U8, name="xq_sc", align_bytes=64)
         nc.vector.tensor_copy(out=xq_sc[:], in_=x_sc[:].indirect(offs_sb[:]))
@@ -106,7 +106,9 @@ def tile_picked_mixhhpgatefdif_none_p_kernel(tc, x_words, x_scales, w1, gn, w2, 
         nc.vector.tensor_copy(out=xh_sc[:].bitcast(I32), in_=xh_raw[:].bitcast(I32))
         for r in (2, 3):
             nc.sync.dma_start(out=xh_sc[:].bitcast(I32)[r:P:32, :], in_=xh_raw[:].bitcast(I32)[16 + r : P : 32, :])
-        w1_q = [quantise(w1_bf[t], P, f"w1_{t}") for t in range(PACK - 1)]
+        n2_sb = load_list(n2, "n2_sb")
+        n3_sb = load_list(n3, "n3_sb")
+        w1_q = [quantise(w1_bf[t], P, f"w1_{t}") for t in range(PACK)]
         xq_wd = keep.tile([P, S], U32, name="xq_wd", align_bytes=64)
         rows = [keep.tile([P, S], F32, name=f"rows{t}") for t in range(PACK)]
         y0_ps = [psum.tile([P, S // 2], F32, name=f"y0_ps{u}", tag=f"y0_ps{u}") for u in range(2)]
@@ -117,7 +119,6 @@ def tile_picked_mixhhpgatefdif_none_p_kernel(tc, x_words, x_scales, w1, gn, w2, 
             product(y0_ps[u][:], w1_q[0], (xq_wd[:, cols], xq_sc[:, cols]), True, True)
             product(y_ps[1][:, cols], w1_q[1], (xq_wd[:, cols], xq_sc[:, cols]), True, True)
             nc.scalar.copy(out=rows[0][:, cols], in_=y0_ps[u][:])
-        w1_q.append(quantise(w1_bf[3], P, "w1_3"))
         for t in range(2, PACK):
             product(y_ps[t][:], w1_q[t], (xq_wd, xq_sc), True, True)
         xh_wd = keep.tile([P, V], U32, name="xh_wd", align_bytes=64)
@@ -178,17 +179,17 @@ def tile_picked_mixhhpgatefdif_none_p_kernel(tc, x_words, x_scales, w1, gn, w2, 
         extremes(1, 0, V)
         w2_q[0] = quantise(w2_bf0, P, "w2_0")
         gain_on(1, 0, V)
-        w3_bf0 = rounded(nc.vector.tensor_copy, w3_raw, 0, "w3_0")
         extremes(2, 0, V)
         extremes(3, 0, HALF)
         gain_on(2, 0, V)
-        w3_q[0] = quantise(w3_bf0, P, "w3_0")
         gain_on(3, 0, HALF)
         extremes(3, HALF, V)
         for u in range(4):
             gate_of(gate[:, :, u * Q : (u + 1) * Q], small[:, :, u * Q : (u + 1) * Q])
+        w3_bf0 = rounded(nc.vector.tensor_copy, w3_raw, 0, "w3_0")
         make_z(0, Q)
         gain_on(3, HALF, V)
+        w3_q[0] = quantise(w3_bf0, P, "w3_0")
         make_z(Q, HALF)
         make_z(HALF, 3 * Q)
         quantise_z(0, HALF)

@@ -59,6 +59,10 @@ def tile_picked_mixhhpgatefdif_none_p_kernel(tc, x_words, x_scales, w1, gn, w2, 
         nc.sync.dma_start(out=w1_raw[:, 2:, :], in_=w1_rows[:, 2:, :])
         x_wd = keep.tile([P, T], U32, name="x_wd", align_bytes=64)
         nc.sync.dma_start(out=x_wd[:].bitcast(I32), in_=x_words[0].rearrange("p n t -> p (n t)").bitcast(I32))
+        warm_in = keep.tile([P, 1], F32, name="warm_in")
+        warm_out = keep.tile([P, 1], F32, name="warm_out")
+        nc.vector.memset(warm_in[:], 0.0)
+        nc.scalar.activation(out=warm_out[:], in_=warm_in[:], func=ACT.Sigmoid)
         n1_sb = load_list(n1, "n1_sb")
         w2_raw = keep.tile([P, PACK, N], F32, name="w2_raw")
         w2_rows = w2.rearrange("(q t r) c -> t q r c", t=PACK, r=8)

@@ -1,6 +1,7 @@
 from contextlib import ExitStack
 
 import concourse.mybir as mybir
+from concourse.masks import make_identity
 
 K, T, S, V, N, H = 512, 2048, 512, 256, 512, 512
 FLOPS = 2 * K * H * S + 2 * H * N * V + 2 * K * N * V
@@ -34,13 +35,10 @@ def tile_picked_mixhhpgatefdif_none_p_kernel(tc, x_words, x_scales, w1, gn, w2, 
 
         x_sc = keep.tile([P, T], U8, name="x_sc", align_bytes=64)
         nc.vector.memset(x_sc[:].bitcast(I32), 0)
-        gains = []
-        gn_rows = gn.rearrange("(q t r) o -> t q r o", t=PACK, r=8)
-        for t in range(PACK):
-            gain = keep.tile([P, 1], F32, name=f"gain{t}")
-            with nc.allow_non_contiguous_dma(reason="one gain a partition"):
-                nc.gpsimd.dma_start(out=gain[:], in_=gn_rows[t])
-            gains.append(gain)
+        identity = keep.tile([P, P], F32, name="identity")
+        make_identity(nc, identity[:])
+        own_place = keep.tile([P, 8], F32, name="own_place")
+        nc.vector.tensor_reduce(out=own_place[:], in_=identity[:].rearrange("p (q r) -> p r q", r=8), axis=mybir.AxisListType.X, op=ALU.add)
         offs_sb = load_list(offs, "offs_sb")
         w1_raw = keep.tile([P, PACK, H], F32, name="w1_raw")
         w1_rows = w1.rearrange("(p j) c -> p j c", j=PACK)
@@ -64,6 +62,11 @@ def tile_picked_mixhhpgatefdif_none_p_kernel(tc, x_words, x_scales, w1, gn, w2, 
         nc.vector.memset(warm_in[:], 0.0)
         nc.scalar.activation(out=warm_out[:], in_=warm_in[:], func=ACT.Sigmoid)
         n1_sb = load_list(n1, "n1_sb")
+        gn_block = keep.tile([P, PACK, 8], F32, name="gn_block")
+        nc.sync.dma_start(
+            out=gn_block[:].rearrange("p t r -> p (t r)"),
+            in_=gn.rearrange("(q c) o -> q (c o)", c=32).unsqueeze(1).to_broadcast([16, 8, 32]),
+        )
         w2_raw = keep.tile([P, PACK, N], F32, name="w2_raw")
         w2_rows = w2.rearrange("(q t r) c -> t q r c", t=PACK, r=8)
         for t in range(PACK):
@@ -115,8 +118,8 @@ def tile_picked_mixhhpgatefdif_none_p_kernel(tc, x_words, x_scales, w1, gn, w2, 
         w1_q = [quantise(w1_bf[t], P, f"w1_{t}") for t in range(PACK)]
         xq_wd = keep.tile([P, S], U32, name="xq_wd", align_bytes=64)
         rows = [keep.tile([P, S], F32, name=f"rows{t}") for t in range(PACK)]
-        y0_ps = [psum.tile([P, S // 2], F32, name=f"y0_ps{u}", tag=f"y0_ps{u}") for u in range(2)]
-        y_ps = {t: psum.tile([P, S], F32, name=f"y_ps{t}") for t in range(1, PACK)}
+        y0_ps = [psum.tile([P, S // 2], F32, name=f"y0_ps{u}", tag=f"bank{u}") for u in range(2)]
+        y_ps = {t: psum.tile([P, S], F32, name=f"y_ps{t}", tag=f"bank{t + 1}") for t in range(1, PACK)}
         for u in range(2):
             cols = slice(u * (S // 2), (u + 1) * (S // 2))
             nc.vector.tensor_copy(out=xq_wd[:, cols], in_=x_wd[:].indirect(offs_sb[:, u * 16 : (u + 1) * 16]))
@@ -127,6 +130,11 @@ def tile_picked_mixhhpgatefdif_none_p_kernel(tc, x_words, x_scales, w1, gn, w2, 
             product(y_ps[t][:], w1_q[t], (xq_wd, xq_sc), True, True)
         xh_wd = keep.tile([P, V], U32, name="xh_wd", align_bytes=64)
         nc.vector.tensor_copy(out=xh_wd[:], in_=x_wd[:].indirect(hz_sb[:]))
+
+        gn_own = keep.tile([P, PACK, 8], F32, name="gn_own")
+        nc.vector.tensor_tensor(out=gn_own[:], in0=gn_block[:], in1=own_place[:].unsqueeze(1).to_broadcast([P, PACK, 8]), op=ALU.mult)
+        gains = keep.tile([P, PACK], F32, name="gains")
+        nc.vector.tensor_reduce(out=gains[:], in_=gn_own[:], axis=mybir.AxisListType.X, op=ALU.add)
 
         big = keep.tile([P, PACK, V], F32, name="big")
         gained = keep.tile([P, PACK, V], F32, name="gained", tag="later", align_bytes=64)
@@ -153,7 +161,7 @@ def tile_picked_mixhhpgatefdif_none_p_kernel(tc, x_words, x_scales, w1, gn, w2, 
             nc.scalar.activation(out=dst, in_=low, func=ACT.Sigmoid)
 
         def gain_on(t, v0, v1):
-            nc.vector.tensor_scalar(out=gained[:, t, v0:v1], in0=big[:, t, v0:v1], scalar1=gains[t][:], scalar2=None, op0=ALU.mult)
+            nc.vector.tensor_scalar(out=gained[:, t, v0:v1], in0=big[:, t, v0:v1], scalar1=gains[:, t : t + 1], scalar2=None, op0=ALU.mult)
 
         def make_z(v0, v1):
             nc.vector.tensor_tensor(
@@ -204,17 +212,19 @@ def tile_picked_mixhhpgatefdif_none_p_kernel(tc, x_words, x_scales, w1, gn, w2, 
         late = keep.tile([P, 3, P, PACK], BF16, name="late_bf", tag="late", align_bytes=64)
 
         out_rows = out.rearrange("(q t r) v -> t q r v", t=PACK, r=8)
-        h_ps = [psum.tile([P, V], F32, name=f"h_ps{t}", tag="y0_ps0" if t == 3 else f"h_ps{t}") for t in range(PACK)]
+        h_ps = {t: psum.tile([P, V], F32, name=f"h_ps{t}", tag=f"bank{t + 4}") for t in range(1, PACK)}
+        h0_ps = [psum.tile([P, HALF], F32, name=f"h0_ps{u}", tag=f"bank{u}") for u in range(2)]
 
         def make_h(t):
             product(h_ps[t][:], w2_q[t], (z_wd, z_sc), True, False)
             product(h_ps[t][:], w3_q[t], (xh_wd, xh_sc), False, True)
 
         def make_first_h():
-            product(h_ps[0][:], w3_q[0], (xh_wd, xh_sc), True, False)
-            for u in range(2):
+            for u, copy in enumerate((nc.scalar.copy, nc.vector.tensor_copy)):
                 cols = slice(u * HALF, (u + 1) * HALF)
-                product(h_ps[0][:, cols], w2_q[0], (z_wd[:, cols], z_sc[:, cols]), False, u == 1)
+                product(h0_ps[u][:], w3_q[0], (xh_wd[:, cols], xh_sc[:, cols]), True, False)
+                product(h0_ps[u][:], w2_q[0], (z_wd[:, cols], z_sc[:, cols]), False, True)
+                copy(out=rows[0][:, cols], in_=h0_ps[u][:])
 
         def fetch_h(t):
             nc.vector.tensor_copy(out=rows[t][:, :V], in_=h_ps[t][:])
@@ -232,7 +242,7 @@ def tile_picked_mixhhpgatefdif_none_p_kernel(tc, x_words, x_scales, w1, gn, w2, 
             fetch(factor[t], t, n3_sb)
 
         def bend(t):
-            nc.vector.tensor_tensor(out=diff[t][:], in0=ahead[t][:], in1=h_ps[t][:], op=ALU.subtract)
+            nc.vector.tensor_tensor(out=diff[t][:], in0=ahead[t][:], in1=h_ps[t][:] if t else rows[0][:, :V], op=ALU.subtract)
             nc.scalar.activation(out=bent[t][:], in_=diff[t][:], func=ACT.Tanh)
 
         def finish(t):
@@ -241,7 +251,6 @@ def tile_picked_mixhhpgatefdif_none_p_kernel(tc, x_words, x_scales, w1, gn, w2, 
             nc.sync.dma_start(out=out_rows[t], in_=result[:])
 
         make_first_h()
-        fetch_h(0)
         look_up(0)
         rounded(nc.scalar.copy, w2_raw, 1, "w2_1", late[:, 0])
         rounded(nc.scalar.copy, w3_raw, 1, "w3_1", late[:, 1])

@@ -15,10 +15,14 @@ U8 = mybir.dt.uint8
 FP8X4 = mybir.dt.float8_e4m3fn_x4
 ALU = mybir.AluOpType
 ACT = mybir.ActivationFunctionType
+INNERMOST = mybir.AxisListType.X
 
 P = 128
 PACK = 4
-HALF = V // 2
+RUN = 8
+GROUP = 16
+LINE = 4
+HALF, QUARTER = V // 2, V // 4
 
 
 def tile_picked_mixhhpgatefdif_none_p_kernel(tc, x_words, x_scales, w1, gn, w2, w3, offs, n1, hz, n2, n3, out):
@@ -34,140 +38,142 @@ def tile_picked_mixhhpgatefdif_none_p_kernel(tc, x_words, x_scales, w1, gn, w2, 
             return held
 
         x_sc = keep.tile([P, T], U8, name="x_sc", align_bytes=64)
-        nc.vector.memset(x_sc[:].bitcast(I32), 0)
+        nc.gpsimd.memset(x_sc[:].bitcast(I32), 0)
+
         identity = keep.tile([P, P], F32, name="identity")
         make_identity(nc, identity[:])
-        own_place = keep.tile([P, 8], F32, name="own_place")
-        nc.vector.tensor_reduce(out=own_place[:], in_=identity[:].rearrange("p (q r) -> p r q", r=8), axis=mybir.AxisListType.X, op=ALU.add)
+        gn_block = keep.tile([P, PACK, RUN], F32, name="gn_block")
+        nc.gpsimd.dma_start(
+            out=gn_block[:].rearrange("p t r -> p (t r)"),
+            in_=gn.rearrange("(q c) o -> q (c o)", c=PACK * RUN).unsqueeze(1).to_broadcast([P // RUN, RUN, PACK * RUN]),
+        )
+        own_place = keep.tile([P, RUN], F32, name="own_place")
+        nc.vector.tensor_reduce(out=own_place[:], in_=identity[:].rearrange("p (q r) -> p r q", r=RUN), axis=INNERMOST, op=ALU.add)
+
         offs_sb = load_list(offs, "offs_sb")
         w1_raw = keep.tile([P, PACK, H], F32, name="w1_raw")
         w1_rows = w1.rearrange("(p j) c -> p j c", j=PACK)
-        nc.sync.dma_start(out=w1_raw[:, :2, :], in_=w1_rows[:, :2, :])
+        nc.sync.dma_start(out=w1_raw[:, : PACK // 2, :], in_=w1_rows[:, : PACK // 2, :])
         x_sc32 = x_sc[:].bitcast(I32)
-        rows32 = x_scales[0].bitcast(I32)
-        for r in range(4):
-            if r < 2:
-                nc.sync.dma_start(out=x_sc32[r:P:32, :], in_=rows32[r:16:4, :])
-            else:
-                nc.sync.dma_start(
-                    out=x_sc32[r:P:16, :],
-                    in_=rows32[r:16:4, :].unsqueeze(1).to_broadcast([4, 2, T // 4]),
-                )
+        scale_rows = x_scales[0].bitcast(I32)
+        for r in (0, 1):
+            nc.sync.dma_start(out=x_sc32[r : P : 2 * GROUP, :], in_=scale_rows[r : K // 32 : 4, :])
+        for r in (2, 3):
+            nc.sync.dma_start(out=x_sc32[r:P:GROUP, :], in_=scale_rows[r : K // 32 : 4, :].unsqueeze(1).to_broadcast([4, 2, T // 4]))
         hz_sb = load_list(hz, "hz_sb")
-        nc.sync.dma_start(out=w1_raw[:, 2:, :], in_=w1_rows[:, 2:, :])
+        nc.sync.dma_start(out=w1_raw[:, PACK // 2 :, :], in_=w1_rows[:, PACK // 2 :, :])
         x_wd = keep.tile([P, T], U32, name="x_wd", align_bytes=64)
         nc.sync.dma_start(out=x_wd[:].bitcast(I32), in_=x_words[0].rearrange("p n t -> p (n t)").bitcast(I32))
+
         warm_in = keep.tile([P, 1], F32, name="warm_in")
         warm_out = keep.tile([P, 1], F32, name="warm_out")
         nc.vector.memset(warm_in[:], 0.0)
         nc.scalar.activation(out=warm_out[:], in_=warm_in[:], func=ACT.Sigmoid)
+
         n1_sb = load_list(n1, "n1_sb")
-        gn_block = keep.tile([P, PACK, 8], F32, name="gn_block")
-        nc.sync.dma_start(
-            out=gn_block[:].rearrange("p t r -> p (t r)"),
-            in_=gn.rearrange("(q c) o -> q (c o)", c=32).unsqueeze(1).to_broadcast([16, 8, 32]),
-        )
         w2_raw = keep.tile([P, PACK, N], F32, name="w2_raw")
-        w2_rows = w2.rearrange("(q t r) c -> t q r c", t=PACK, r=8)
+        w2_rows = w2.rearrange("(q t r) c -> t q r c", t=PACK, r=RUN)
         for t in range(PACK):
             nc.sync.dma_start(out=w2_raw[:, t, :], in_=w2_rows[t])
         w3_raw = keep.tile([P, PACK, N], F32, name="w3_raw")
         nc.sync.dma_start(out=w3_raw[:], in_=w3.rearrange("(p j) c -> p j c", j=PACK))
 
-        def deal(copy, dst, raw, t):
+        def round_columns(copy, raw, t, dst):
             copy(
-                out=dst.rearrange("p (q a i) j -> p q a j i", a=2, i=4),
-                in_=raw.rearrange("p j (q t a i) -> p t q a j i", t=PACK, a=2, i=4)[:, t],
+                out=dst.rearrange("p (q a i) j -> p q a j i", a=RUN // LINE, i=LINE),
+                in_=raw[:].rearrange("p j (q t a i) -> p t q a j i", t=PACK, a=RUN // LINE, i=LINE)[:, t],
             )
+            return dst
 
-        def quantise(grouped, width, name):
-            codes = keep.tile([P, width], U32, name=name + "_codes", align_bytes=64)
-            scales = keep.tile([P, width], U8, name=name + "_scales", align_bytes=64)
-            nc.vector.quantize_mx(out=codes[:].bitcast(FP8X4), scales=scales[:], in_=grouped.rearrange("p c j -> p (c j)"))
+        def staging(name):
+            return keep.tile([P, P, PACK], BF16, name=name + "_bf", align_bytes=64)[:]
+
+        def quantise(rounded, name):
+            codes = keep.tile([P, P], U32, name=name + "_codes", tag=name + "_codes", align_bytes=64)
+            scales = keep.tile([P, P], U8, name=name + "_scales", tag=name + "_scales", align_bytes=64)
+            nc.vector.quantize_mx(out=codes[:].bitcast(FP8X4), scales=scales[:], in_=rounded.rearrange("p c j -> p (c j)"))
             return codes, scales
 
-        def product(acc, weights, moving, start, stop):
+        def product(acc, weights, words, scales, start, stop):
             nc.tensor.matmul_mx(
                 out=acc,
                 lhsT=weights[0][:].bitcast(FP8X4),
                 lhsT_scale=weights[1][:],
-                rhs=moving[0][:].bitcast(FP8X4),
-                rhs_scale=moving[1][:],
+                rhs=words.bitcast(FP8X4),
+                rhs_scale=scales,
                 start=start,
                 stop=stop,
             )
 
-        def rounded(copy, raw, t, name, dst=None):
-            if dst is None:
-                dst = keep.tile([P, P, PACK], BF16, name=name + "_bf", align_bytes=64)[:]
-            deal(copy, dst, raw[:], t)
-            return dst
-
-        w1_bf = [rounded(nc.scalar.copy if t < 3 else nc.vector.tensor_copy, w1_raw, t, f"w1_{t}") for t in range(PACK)]
-
+        w1_bf = [
+            round_columns(nc.scalar.copy if t < PACK - 1 else nc.vector.tensor_copy, w1_raw, t, staging(f"w1_{t}"))
+            for t in range(PACK)
+        ]
         xq_sc = keep.tile([P, S], U8, name="xq_sc", align_bytes=64)
         nc.vector.tensor_copy(out=xq_sc[:], in_=x_sc[:].indirect(offs_sb[:]))
-        xh_raw = keep.tile([P, V], U8, name="xh_raw", align_bytes=64)
-        nc.vector.tensor_copy(out=xh_raw[:], in_=x_sc[:].indirect(hz_sb[:]))
-        xh_sc = keep.tile([P, V], U8, name="xh_sc", align_bytes=64)
-        nc.vector.tensor_copy(out=xh_sc[:].bitcast(I32), in_=xh_raw[:].bitcast(I32))
-        for r in (2, 3):
-            nc.sync.dma_start(out=xh_sc[:].bitcast(I32)[r:P:32, :], in_=xh_raw[:].bitcast(I32)[16 + r : P : 32, :])
-        n2_sb = load_list(n2, "n2_sb")
-        n3_sb = load_list(n3, "n3_sb")
-        w1_q = [quantise(w1_bf[t], P, f"w1_{t}") for t in range(PACK)]
+        xh_gathered = keep.tile([P, V], U8, name="xh_gathered", align_bytes=64)
+        nc.vector.tensor_copy(out=xh_gathered[:], in_=x_sc[:].indirect(hz_sb[:]))
+        w1_q = [quantise(w1_bf[t], f"w1_{t}") for t in range(PACK)]
+
         xq_wd = keep.tile([P, S], U32, name="xq_wd", align_bytes=64)
-        rows = [keep.tile([P, S], F32, name=f"rows{t}") for t in range(PACK)]
+        window = [keep.tile([P, S], F32, name=f"window{t}") for t in range(PACK)]
         y0_ps = [psum.tile([P, S // 2], F32, name=f"y0_ps{u}", tag=f"bank{u}") for u in range(2)]
         y_ps = {t: psum.tile([P, S], F32, name=f"y_ps{t}", tag=f"bank{t + 1}") for t in range(1, PACK)}
         for u in range(2):
             cols = slice(u * (S // 2), (u + 1) * (S // 2))
-            nc.vector.tensor_copy(out=xq_wd[:, cols], in_=x_wd[:].indirect(offs_sb[:, u * 16 : (u + 1) * 16]))
-            product(y0_ps[u][:], w1_q[0], (xq_wd[:, cols], xq_sc[:, cols]), True, True)
-            product(y_ps[1][:, cols], w1_q[1], (xq_wd[:, cols], xq_sc[:, cols]), True, True)
-            nc.scalar.copy(out=rows[0][:, cols], in_=y0_ps[u][:])
+            nc.vector.tensor_copy(out=xq_wd[:, cols], in_=x_wd[:].indirect(offs_sb[:, cols.start // GROUP : cols.stop // GROUP]))
+            product(y0_ps[u][:], w1_q[0], xq_wd[:, cols], xq_sc[:, cols], True, True)
+            product(y_ps[1][:, cols], w1_q[1], xq_wd[:, cols], xq_sc[:, cols], True, True)
+            nc.scalar.copy(out=window[0][:, cols], in_=y0_ps[u][:])
         for t in range(2, PACK):
-            product(y_ps[t][:], w1_q[t], (xq_wd, xq_sc), True, True)
+            product(y_ps[t][:], w1_q[t], xq_wd[:], xq_sc[:], True, True)
+
         xh_wd = keep.tile([P, V], U32, name="xh_wd", align_bytes=64)
         nc.vector.tensor_copy(out=xh_wd[:], in_=x_wd[:].indirect(hz_sb[:]))
-
-        gn_own = keep.tile([P, PACK, 8], F32, name="gn_own")
-        nc.vector.tensor_tensor(out=gn_own[:], in0=gn_block[:], in1=own_place[:].unsqueeze(1).to_broadcast([P, PACK, 8]), op=ALU.mult)
+        xh_sc = keep.tile([P, V], U8, name="xh_sc", tag="w1_0_scales", align_bytes=64)
+        nc.vector.tensor_copy(out=xh_sc[:].bitcast(I32), in_=xh_gathered[:].bitcast(I32))
+        for r in (2, 3):
+            nc.sync.dma_start(
+                out=xh_sc[:].bitcast(I32)[r : P : 2 * GROUP, :],
+                in_=xh_gathered[:].bitcast(I32)[GROUP + r : P : 2 * GROUP, :],
+            )
+        n2_sb = load_list(n2, "n2_sb")
+        n3_sb = load_list(n3, "n3_sb")
+        gn_own = keep.tile([P, PACK, RUN], F32, name="gn_own", tag="w1_0_codes", align_bytes=64)
+        nc.vector.tensor_tensor(out=gn_own[:], in0=gn_block[:], in1=own_place[:].unsqueeze(1).to_broadcast([P, PACK, RUN]), op=ALU.mult)
         gains = keep.tile([P, PACK], F32, name="gains")
-        nc.vector.tensor_reduce(out=gains[:], in_=gn_own[:], axis=mybir.AxisListType.X, op=ALU.add)
+        nc.vector.tensor_reduce(out=gains[:], in_=gn_own[:], axis=INNERMOST, op=ALU.add)
 
-        big = keep.tile([P, PACK, V], F32, name="big")
-        gained = keep.tile([P, PACK, V], F32, name="gained", tag="later", align_bytes=64)
+        larger = keep.tile([P, PACK, V], F32, name="larger")
+        gained = keep.tile([P, PACK, V], F32, name="gained", tag="after_z", align_bytes=64)
         gate = keep.tile([P, PACK, V], F32, name="gate")
-        small = keep.tile([P, PACK, V], F32, name="small", tag="late", align_bytes=64)
+        smaller = keep.tile([P, PACK, V], F32, name="smaller", tag="after_gates", align_bytes=64)
         z_bf = keep.tile([P, V, PACK], BF16, name="z_bf", align_bytes=64)
         z_wd = keep.tile([P, V], U32, name="z_wd", align_bytes=64)
         z_sc = keep.tile([P, V], U8, name="z_sc", align_bytes=64)
+        for t in range(1, PACK):
+            nc.vector.tensor_copy(out=window[t][:], in_=y_ps[t][:])
+        lined = keep.tile([P, PACK, V, 2], F32, name="lined")
 
-        def line_up(lined, t, v0, v1):
-            nc.scalar.activation(
-                out=lined.rearrange("p v e -> p (v e)"),
-                in_=rows[t][:].indirect(n1_sb[:, v0 // 8 : v1 // 8]),
-                func=ACT.Copy,
-            )
+        def extremes(t, v0, v1):
+            for a in range(v0, v1, HALF):
+                nc.scalar.activation(
+                    out=lined[:, t, a : a + HALF].rearrange("p v e -> p (v e)"),
+                    in_=window[t][:].indirect(n1_sb[:, 2 * a // GROUP : 2 * (a + HALF) // GROUP]),
+                    func=ACT.Copy,
+                )
+            first, second = lined[:, t : t + 1, v0:v1, 0], lined[:, t : t + 1, v0:v1, 1]
+            nc.vector.tensor_tensor(out=smaller[:, t : t + 1, v0:v1], in0=first, in1=second, op=ALU.min)
+            nc.vector.tensor_tensor(out=larger[:, t : t + 1, v0:v1], in0=first, in1=second, op=ALU.max)
 
-        def smaller(low, lined):
-            nc.vector.tensor_tensor(out=low, in0=lined[:, :, :, 0], in1=lined[:, :, :, 1], op=ALU.min)
-
-        def larger(high, lined):
-            nc.vector.tensor_tensor(out=high, in0=lined[:, :, :, 0], in1=lined[:, :, :, 1], op=ALU.max)
-
-        def gate_of(dst, low):
-            nc.scalar.activation(out=dst, in_=low, func=ACT.Sigmoid)
-
-        def gain_on(t, v0, v1):
-            nc.vector.tensor_scalar(out=gained[:, t, v0:v1], in0=big[:, t, v0:v1], scalar1=gains[:, t : t + 1], scalar2=None, op0=ALU.mult)
+        def apply_gain(t, v0, v1):
+            nc.vector.tensor_scalar(out=gained[:, t, v0:v1], in0=larger[:, t, v0:v1], scalar1=gains[:, t : t + 1], scalar2=None, op0=ALU.mult)
 
         def make_z(v0, v1):
             nc.vector.tensor_tensor(
-                out=z_bf[:, v0:v1, :].rearrange("p (c i) t -> p c t i", i=4),
-                in0=gained[:, :, v0:v1].rearrange("p t (c i) -> p c t i", i=4),
-                in1=gate[:, :, v0:v1].rearrange("p t (c i) -> p c t i", i=4),
+                out=z_bf[:, v0:v1, :].rearrange("p (c i) t -> p c t i", i=LINE),
+                in0=gained[:, :, v0:v1].rearrange("p t (c i) -> p c t i", i=LINE),
+                in1=gate[:, :, v0:v1].rearrange("p t (c i) -> p c t i", i=LINE),
                 op=ALU.mult,
             )
 
@@ -175,109 +181,91 @@ def tile_picked_mixhhpgatefdif_none_p_kernel(tc, x_words, x_scales, w1, gn, w2, 
             nc.vector.quantize_mx(out=z_wd[:, v0:v1].bitcast(FP8X4), scales=z_sc[:, v0:v1], in_=z_bf[:, v0:v1, :].rearrange("p c j -> p (c j)"))
 
         w2_q, w3_q = {}, {}
-        Q = V // 4
-        for t in range(1, PACK):
-            nc.vector.tensor_copy(out=rows[t][:], in_=y_ps[t][:])
-        lined = keep.tile([P, PACK, V, 2], F32, name="lined")
-
-        def extremes(t, v0, v1):
-            line_up(lined[:, t, v0:v1], t, v0, v1) if v1 - v0 == HALF else [line_up(lined[:, t, a : a + HALF], t, a, a + HALF) for a in (0, HALF)]
-            smaller(small[:, t : t + 1, v0:v1], lined[:, t : t + 1, v0:v1])
-            larger(big[:, t : t + 1, v0:v1], lined[:, t : t + 1, v0:v1])
-
         extremes(0, 0, V)
-        w2_bf0 = rounded(nc.vector.tensor_copy, w2_raw, 0, "w2_0")
-        gain_on(0, 0, V)
+        w2_bf0 = round_columns(nc.vector.tensor_copy, w2_raw, 0, staging("w2_0"))
+        apply_gain(0, 0, V)
         extremes(1, 0, V)
-        w2_q[0] = quantise(w2_bf0, P, "w2_0")
-        gain_on(1, 0, V)
+        w2_q[0] = quantise(w2_bf0, "w2_0")
+        apply_gain(1, 0, V)
         extremes(2, 0, V)
         extremes(3, 0, HALF)
-        gain_on(2, 0, V)
-        gain_on(3, 0, HALF)
+        apply_gain(2, 0, V)
+        apply_gain(3, 0, HALF)
         extremes(3, HALF, V)
-        for u in range(4):
-            gate_of(gate[:, :, u * Q : (u + 1) * Q], small[:, :, u * Q : (u + 1) * Q])
-        w3_bf0 = rounded(nc.vector.tensor_copy, w3_raw, 0, "w3_0")
-        make_z(0, Q)
-        gain_on(3, HALF, V)
-        w3_q[0] = quantise(w3_bf0, P, "w3_0")
-        make_z(Q, HALF)
-        make_z(HALF, 3 * Q)
+        for v0 in range(0, V, QUARTER):
+            nc.scalar.activation(out=gate[:, :, v0 : v0 + QUARTER], in_=smaller[:, :, v0 : v0 + QUARTER], func=ACT.Sigmoid)
+        w3_bf0 = round_columns(nc.vector.tensor_copy, w3_raw, 0, staging("w3_0"))
+        make_z(0, QUARTER)
+        apply_gain(3, HALF, V)
+        w3_q[0] = quantise(w3_bf0, "w3_0")
+        make_z(QUARTER, HALF)
+        make_z(HALF, V - QUARTER)
         quantise_z(0, HALF)
-        make_z(3 * Q, V)
-        quantise_z(HALF, 3 * Q)
-        quantise_z(3 * Q, V)
-        later = keep.tile([P, 3, P, PACK], BF16, name="later_bf", tag="later", align_bytes=64)
-        late = keep.tile([P, 3, P, PACK], BF16, name="late_bf", tag="late", align_bytes=64)
+        make_z(V - QUARTER, V)
+        quantise_z(HALF, V - QUARTER)
+        quantise_z(V - QUARTER, V)
 
-        out_rows = out.rearrange("(q t r) v -> t q r v", t=PACK, r=8)
-        h_ps = {t: psum.tile([P, V], F32, name=f"h_ps{t}", tag=f"bank{t + 4}") for t in range(1, PACK)}
+        by_vector = keep.tile([P, 3, P, PACK], BF16, name="by_vector", tag="after_z", align_bytes=64)
+        by_scalar = keep.tile([P, 3, P, PACK], BF16, name="by_scalar", tag="after_gates", align_bytes=64)
+
+        out_rows = out.rearrange("(q t r) v -> t q r v", t=PACK, r=RUN)
+        h_ps = {t: psum.tile([P, V], F32, name=f"h_ps{t}", tag=f"bank{t + PACK}") for t in range(1, PACK)}
         h0_ps = [psum.tile([P, HALF], F32, name=f"h0_ps{u}", tag=f"bank{u}") for u in range(2)]
-
-        def make_h(t):
-            product(h_ps[t][:], w2_q[t], (z_wd, z_sc), True, False)
-            product(h_ps[t][:], w3_q[t], (xh_wd, xh_sc), False, True)
-
-        def make_first_h():
-            for u, copy in enumerate((nc.scalar.copy, nc.vector.tensor_copy)):
-                cols = slice(u * HALF, (u + 1) * HALF)
-                product(h0_ps[u][:], w3_q[0], (xh_wd[:, cols], xh_sc[:, cols]), True, False)
-                product(h0_ps[u][:], w2_q[0], (z_wd[:, cols], z_sc[:, cols]), False, True)
-                copy(out=rows[0][:, cols], in_=h0_ps[u][:])
-
-        def fetch_h(t):
-            nc.vector.tensor_copy(out=rows[t][:, :V], in_=h_ps[t][:])
-
-        ahead = [keep.tile([P, V], F32, name=f"ahead{t}") for t in range(PACK)]
-        factor = [keep.tile([P, V], F32, name=f"factor{t}") for t in range(PACK)]
+        at_n2 = [keep.tile([P, V], F32, name=f"at_n2_{t}") for t in range(PACK)]
+        at_n3 = [keep.tile([P, V], F32, name=f"at_n3_{t}") for t in range(PACK)]
         diff = [keep.tile([P, V], F32, name=f"diff{t}") for t in range(PACK)]
         bent = [keep.tile([P, V], F32, name=f"bent{t}") for t in range(PACK)]
 
-        def fetch(dst, t, offsets):
-            nc.scalar.activation(out=dst[:], in_=rows[t][:].indirect(offsets[:]), func=ACT.Copy)
+        def make_h(t):
+            product(h_ps[t][:], w2_q[t], z_wd[:], z_sc[:], True, False)
+            product(h_ps[t][:], w3_q[t], xh_wd[:], xh_sc[:], False, True)
 
-        def look_up(t):
-            fetch(ahead[t], t, n2_sb)
-            fetch(factor[t], t, n3_sb)
+        def gather_h(t):
+            for dst, offsets in ((at_n2[t], n2_sb), (at_n3[t], n3_sb)):
+                nc.scalar.activation(out=dst[:], in_=window[t][:].indirect(offsets[:]), func=ACT.Copy)
 
-        def bend(t):
-            nc.vector.tensor_tensor(out=diff[t][:], in0=ahead[t][:], in1=h_ps[t][:] if t else rows[0][:, :V], op=ALU.subtract)
+        def empty_and_gather(t):
+            nc.vector.tensor_copy(out=window[t][:, :V], in_=h_ps[t][:])
+            gather_h(t)
+
+        def bend(t, h):
+            nc.vector.tensor_tensor(out=diff[t][:], in0=at_n2[t][:], in1=h, op=ALU.subtract)
             nc.scalar.activation(out=bent[t][:], in_=diff[t][:], func=ACT.Tanh)
 
         def finish(t):
             result = keep.tile([P, V], F32, name=f"result{t}")
-            nc.vector.tensor_tensor(out=result[:], in0=bent[t][:], in1=factor[t][:], op=ALU.mult)
+            nc.vector.tensor_tensor(out=result[:], in0=bent[t][:], in1=at_n3[t][:], op=ALU.mult)
             nc.sync.dma_start(out=out_rows[t], in_=result[:])
 
-        make_first_h()
-        look_up(0)
-        rounded(nc.scalar.copy, w2_raw, 1, "w2_1", late[:, 0])
-        rounded(nc.scalar.copy, w3_raw, 1, "w3_1", late[:, 1])
-        rounded(nc.scalar.copy, w3_raw, 2, "w3_2", late[:, 2])
-        rounded(nc.vector.tensor_copy, w2_raw, 2, "w2_2", later[:, 0])
-        w2_q[1] = quantise(late[:, 0], P, "w2_1")
-        w3_q[1] = quantise(late[:, 1], P, "w3_1")
+        for u, copy in enumerate((nc.scalar.copy, nc.vector.tensor_copy)):
+            cols = slice(u * HALF, (u + 1) * HALF)
+            product(h0_ps[u][:], w3_q[0], xh_wd[:, cols], xh_sc[:, cols], True, False)
+            product(h0_ps[u][:], w2_q[0], z_wd[:, cols], z_sc[:, cols], False, True)
+            copy(out=window[0][:, cols], in_=h0_ps[u][:])
+        gather_h(0)
+
+        round_columns(nc.scalar.copy, w2_raw, 1, by_scalar[:, 0])
+        round_columns(nc.scalar.copy, w3_raw, 1, by_scalar[:, 1])
+        round_columns(nc.scalar.copy, w3_raw, 2, by_scalar[:, 2])
+        round_columns(nc.vector.tensor_copy, w2_raw, 2, by_vector[:, 0])
+        w2_q[1] = quantise(by_scalar[:, 0], "w2_1")
+        w3_q[1] = quantise(by_scalar[:, 1], "w3_1")
         make_h(1)
-        w2_q[2] = quantise(later[:, 0], P, "w2_2")
-        w3_q[2] = quantise(late[:, 2], P, "w3_2")
+        w2_q[2] = quantise(by_vector[:, 0], "w2_2")
+        w3_q[2] = quantise(by_scalar[:, 2], "w3_2")
         make_h(2)
-        fetch_h(1)
-        look_up(1)
-        rounded(nc.vector.tensor_copy, w2_raw, 3, "w2_3", later[:, 1])
-        rounded(nc.vector.tensor_copy, w3_raw, 3, "w3_3", later[:, 2])
-        bend(0)
-        w2_q[3] = quantise(later[:, 1], P, "w2_3")
-        w3_q[3] = quantise(later[:, 2], P, "w3_3")
+        empty_and_gather(1)
+        round_columns(nc.vector.tensor_copy, w2_raw, 3, by_vector[:, 1])
+        round_columns(nc.vector.tensor_copy, w3_raw, 3, by_vector[:, 2])
+        bend(0, window[0][:, :V])
+        w2_q[3] = quantise(by_vector[:, 1], "w2_3")
+        w3_q[3] = quantise(by_vector[:, 2], "w3_3")
         make_h(3)
-        fetch_h(2)
-        look_up(2)
-        bend(1)
-        fetch_h(3)
-        look_up(3)
-        finish(0)
-        bend(2)
-        finish(1)
-        bend(3)
-        finish(2)
-        finish(3)
+        empty_and_gather(2)
+        bend(1, h_ps[1][:])
+        empty_and_gather(3)
+        for t in range(2, PACK):
+            finish(t - 2)
+            bend(t, h_ps[t][:])
+        for t in range(PACK - 2, PACK):
+            finish(t)

from contextlib import ExitStack

import concourse.mybir as mybir
from concourse.masks import make_identity

K, T, S, V, N, H = 512, 2048, 512, 256, 512, 512
FLOPS = 2 * K * H * S + 2 * H * N * V + 2 * K * N * V

F32 = mybir.dt.float32
BF16 = mybir.dt.bfloat16
I32 = mybir.dt.int32
U32 = mybir.dt.uint32
U16 = mybir.dt.uint16
U8 = mybir.dt.uint8
FP8X4 = mybir.dt.float8_e4m3fn_x4
ALU = mybir.AluOpType
ACT = mybir.ActivationFunctionType
INNERMOST = mybir.AxisListType.X

P = 128
PACK = 4
RUN = 8
GROUP = 16
LINE = 4
HALF, QUARTER = V // 2, V // 4


def tile_picked_mixhhpgatefdif_none_p_kernel(tc, x_words, x_scales, w1, gn, w2, w3, offs, n1, hz, n2, n3, out):
    nc = tc.nc
    with ExitStack() as ctx:
        lists = ctx.enter_context(tc.tile_pool(name="lists", bufs=1))
        keep = ctx.enter_context(tc.tile_pool(name="keep", bufs=1))
        psum = ctx.enter_context(tc.psum_pool(name="psum", bufs=1))

        def load_list(src, name):
            held = lists.tile(list(src.shape), U16, name=name)
            nc.sync.dma_start(out=held[:], in_=src)
            return held

        x_sc = keep.tile([P, T], U8, name="x_sc", align_bytes=64)
        nc.gpsimd.memset(x_sc[:].bitcast(I32), 0)

        identity = keep.tile([P, P], F32, name="identity")
        make_identity(nc, identity[:])
        gn_block = keep.tile([P, PACK, RUN], F32, name="gn_block")
        nc.gpsimd.dma_start(
            out=gn_block[:].rearrange("p t r -> p (t r)"),
            in_=gn.rearrange("(q c) o -> q (c o)", c=PACK * RUN).unsqueeze(1).to_broadcast([P // RUN, RUN, PACK * RUN]),
        )
        own_place = keep.tile([P, RUN], F32, name="own_place")
        nc.vector.tensor_reduce(out=own_place[:], in_=identity[:].rearrange("p (q r) -> p r q", r=RUN), axis=INNERMOST, op=ALU.add)

        offs_sb = load_list(offs, "offs_sb")
        w1_raw = keep.tile([P, PACK, H], F32, name="w1_raw")
        w1_rows = w1.rearrange("(p j) c -> p j c", j=PACK)
        nc.sync.dma_start(out=w1_raw[:, : PACK // 2, :], in_=w1_rows[:, : PACK // 2, :])
        x_sc32 = x_sc[:].bitcast(I32)
        scale_rows = x_scales[0].bitcast(I32)
        for r in (0, 1):
            nc.sync.dma_start(out=x_sc32[r : P : 2 * GROUP, :], in_=scale_rows[r : K // 32 : 4, :])
        for r in (2, 3):
            nc.sync.dma_start(out=x_sc32[r:P:GROUP, :], in_=scale_rows[r : K // 32 : 4, :].unsqueeze(1).to_broadcast([4, 2, T // 4]))
        hz_sb = load_list(hz, "hz_sb")
        nc.sync.dma_start(out=w1_raw[:, PACK // 2 :, :], in_=w1_rows[:, PACK // 2 :, :])
        x_wd = keep.tile([P, T], U32, name="x_wd", align_bytes=64)
        nc.sync.dma_start(out=x_wd[:].bitcast(I32), in_=x_words[0].rearrange("p n t -> p (n t)").bitcast(I32))

        warm_in = keep.tile([P, 1], F32, name="warm_in")
        warm_out = keep.tile([P, 1], F32, name="warm_out")
        nc.vector.memset(warm_in[:], 0.0)
        nc.scalar.activation(out=warm_out[:], in_=warm_in[:], func=ACT.Sigmoid)

        n1_sb = load_list(n1, "n1_sb")
        w2_raw = keep.tile([P, PACK, N], F32, name="w2_raw")
        w2_rows = w2.rearrange("(q t r) c -> t q r c", t=PACK, r=RUN)
        for t in range(PACK):
            nc.sync.dma_start(out=w2_raw[:, t, :], in_=w2_rows[t])
        w3_raw = keep.tile([P, PACK, N], F32, name="w3_raw")
        nc.sync.dma_start(out=w3_raw[:], in_=w3.rearrange("(p j) c -> p j c", j=PACK))

        def round_columns(copy, raw, t, dst):
            copy(
                out=dst.rearrange("p (q a i) j -> p q a j i", a=RUN // LINE, i=LINE),
                in_=raw[:].rearrange("p j (q t a i) -> p t q a j i", t=PACK, a=RUN // LINE, i=LINE)[:, t],
            )
            return dst

        def staging(name):
            return keep.tile([P, P, PACK], BF16, name=name + "_bf", align_bytes=64)[:]

        def quantise(rounded, name):
            codes = keep.tile([P, P], U32, name=name + "_codes", tag=name + "_codes", align_bytes=64)
            scales = keep.tile([P, P], U8, name=name + "_scales", tag=name + "_scales", align_bytes=64)
            nc.vector.quantize_mx(out=codes[:].bitcast(FP8X4), scales=scales[:], in_=rounded.rearrange("p c j -> p (c j)"))
            return codes, scales

        def product(acc, weights, words, scales, start, stop):
            nc.tensor.matmul_mx(
                out=acc,
                lhsT=weights[0][:].bitcast(FP8X4),
                lhsT_scale=weights[1][:],
                rhs=words.bitcast(FP8X4),
                rhs_scale=scales,
                start=start,
                stop=stop,
            )

        w1_bf = [
            round_columns(nc.scalar.copy if t < PACK - 1 else nc.vector.tensor_copy, w1_raw, t, staging(f"w1_{t}"))
            for t in range(PACK)
        ]
        xq_sc = keep.tile([P, S], U8, name="xq_sc", align_bytes=64)
        nc.vector.tensor_copy(out=xq_sc[:], in_=x_sc[:].indirect(offs_sb[:]))
        xh_gathered = keep.tile([P, V], U8, name="xh_gathered", align_bytes=64)
        nc.vector.tensor_copy(out=xh_gathered[:], in_=x_sc[:].indirect(hz_sb[:]))
        w1_q = [quantise(w1_bf[t], f"w1_{t}") for t in range(PACK)]

        xq_wd = keep.tile([P, S], U32, name="xq_wd", align_bytes=64)
        window = [keep.tile([P, S], F32, name=f"window{t}") for t in range(PACK)]
        y0_ps = [psum.tile([P, S // 2], F32, name=f"y0_ps{u}", tag=f"bank{u}") for u in range(2)]
        y_ps = {t: psum.tile([P, S], F32, name=f"y_ps{t}", tag=f"bank{t + 1}") for t in range(1, PACK)}
        for u in range(2):
            cols = slice(u * (S // 2), (u + 1) * (S // 2))
            nc.vector.tensor_copy(out=xq_wd[:, cols], in_=x_wd[:].indirect(offs_sb[:, cols.start // GROUP : cols.stop // GROUP]))
            product(y0_ps[u][:], w1_q[0], xq_wd[:, cols], xq_sc[:, cols], True, True)
            product(y_ps[1][:, cols], w1_q[1], xq_wd[:, cols], xq_sc[:, cols], True, True)
            nc.scalar.copy(out=window[0][:, cols], in_=y0_ps[u][:])
        for t in range(2, PACK):
            product(y_ps[t][:], w1_q[t], xq_wd[:], xq_sc[:], True, True)

        xh_wd = keep.tile([P, V], U32, name="xh_wd", align_bytes=64)
        nc.vector.tensor_copy(out=xh_wd[:], in_=x_wd[:].indirect(hz_sb[:]))
        xh_sc = keep.tile([P, V], U8, name="xh_sc", tag="w1_0_scales", align_bytes=64)
        nc.vector.tensor_copy(out=xh_sc[:].bitcast(I32), in_=xh_gathered[:].bitcast(I32))
        for r in (2, 3):
            nc.sync.dma_start(
                out=xh_sc[:].bitcast(I32)[r : P : 2 * GROUP, :],
                in_=xh_gathered[:].bitcast(I32)[GROUP + r : P : 2 * GROUP, :],
            )
        n2_sb = load_list(n2, "n2_sb")
        n3_sb = load_list(n3, "n3_sb")
        gn_own = keep.tile([P, PACK, RUN], F32, name="gn_own", tag="w1_0_codes", align_bytes=64)
        nc.vector.tensor_tensor(out=gn_own[:], in0=gn_block[:], in1=own_place[:].unsqueeze(1).to_broadcast([P, PACK, RUN]), op=ALU.mult)
        gains = keep.tile([P, PACK], F32, name="gains")
        nc.vector.tensor_reduce(out=gains[:], in_=gn_own[:], axis=INNERMOST, op=ALU.add)

        larger = keep.tile([P, PACK, V], F32, name="larger")
        gained = keep.tile([P, PACK, V], F32, name="gained", tag="after_z", align_bytes=64)
        gate = keep.tile([P, PACK, V], F32, name="gate")
        smaller = keep.tile([P, PACK, V], F32, name="smaller", tag="after_gates", align_bytes=64)
        z_bf = keep.tile([P, V, PACK], BF16, name="z_bf", align_bytes=64)
        z_wd = keep.tile([P, V], U32, name="z_wd", align_bytes=64)
        z_sc = keep.tile([P, V], U8, name="z_sc", align_bytes=64)
        for t in range(1, PACK):
            nc.vector.tensor_copy(out=window[t][:], in_=y_ps[t][:])
        lined = keep.tile([P, PACK, V, 2], F32, name="lined")

        def extremes(t, v0, v1):
            for a in range(v0, v1, HALF):
                nc.scalar.activation(
                    out=lined[:, t, a : a + HALF].rearrange("p v e -> p (v e)"),
                    in_=window[t][:].indirect(n1_sb[:, 2 * a // GROUP : 2 * (a + HALF) // GROUP]),
                    func=ACT.Copy,
                )
            first, second = lined[:, t : t + 1, v0:v1, 0], lined[:, t : t + 1, v0:v1, 1]
            nc.vector.tensor_tensor(out=smaller[:, t : t + 1, v0:v1], in0=first, in1=second, op=ALU.min)
            nc.vector.tensor_tensor(out=larger[:, t : t + 1, v0:v1], in0=first, in1=second, op=ALU.max)

        def apply_gain(t, v0, v1):
            nc.vector.tensor_scalar(out=gained[:, t, v0:v1], in0=larger[:, t, v0:v1], scalar1=gains[:, t : t + 1], scalar2=None, op0=ALU.mult)

        def make_z(v0, v1):
            nc.vector.tensor_tensor(
                out=z_bf[:, v0:v1, :].rearrange("p (c i) t -> p c t i", i=LINE),
                in0=gained[:, :, v0:v1].rearrange("p t (c i) -> p c t i", i=LINE),
                in1=gate[:, :, v0:v1].rearrange("p t (c i) -> p c t i", i=LINE),
                op=ALU.mult,
            )

        def quantise_z(v0, v1):
            nc.vector.quantize_mx(out=z_wd[:, v0:v1].bitcast(FP8X4), scales=z_sc[:, v0:v1], in_=z_bf[:, v0:v1, :].rearrange("p c j -> p (c j)"))

        w2_q, w3_q = {}, {}
        extremes(0, 0, V)
        w2_bf0 = round_columns(nc.vector.tensor_copy, w2_raw, 0, staging("w2_0"))
        apply_gain(0, 0, V)
        extremes(1, 0, V)
        w2_q[0] = quantise(w2_bf0, "w2_0")
        apply_gain(1, 0, V)
        extremes(2, 0, V)
        extremes(3, 0, HALF)
        apply_gain(2, 0, V)
        apply_gain(3, 0, HALF)
        extremes(3, HALF, V)
        for v0 in range(0, V, QUARTER):
            nc.scalar.activation(out=gate[:, :, v0 : v0 + QUARTER], in_=smaller[:, :, v0 : v0 + QUARTER], func=ACT.Sigmoid)
        w3_bf0 = round_columns(nc.vector.tensor_copy, w3_raw, 0, staging("w3_0"))
        make_z(0, QUARTER)
        apply_gain(3, HALF, V)
        w3_q[0] = quantise(w3_bf0, "w3_0")
        make_z(QUARTER, HALF)
        make_z(HALF, V - QUARTER)
        quantise_z(0, HALF)
        make_z(V - QUARTER, V)
        quantise_z(HALF, V - QUARTER)
        quantise_z(V - QUARTER, V)

        by_vector = keep.tile([P, 3, P, PACK], BF16, name="by_vector", tag="after_z", align_bytes=64)
        by_scalar = keep.tile([P, 3, P, PACK], BF16, name="by_scalar", tag="after_gates", align_bytes=64)

        out_rows = out.rearrange("(q t r) v -> t q r v", t=PACK, r=RUN)
        h_ps = {t: psum.tile([P, V], F32, name=f"h_ps{t}", tag=f"bank{t + PACK}") for t in range(1, PACK)}
        h0_ps = [psum.tile([P, HALF], F32, name=f"h0_ps{u}", tag=f"bank{u}") for u in range(2)]
        at_n2 = [keep.tile([P, V], F32, name=f"at_n2_{t}") for t in range(PACK)]
        at_n3 = [keep.tile([P, V], F32, name=f"at_n3_{t}") for t in range(PACK)]
        diff = [keep.tile([P, V], F32, name=f"diff{t}") for t in range(PACK)]
        bent = [keep.tile([P, V], F32, name=f"bent{t}") for t in range(PACK)]

        def make_h(t):
            product(h_ps[t][:], w2_q[t], z_wd[:], z_sc[:], True, False)
            product(h_ps[t][:], w3_q[t], xh_wd[:], xh_sc[:], False, True)

        def gather_h(t):
            for dst, offsets in ((at_n2[t], n2_sb), (at_n3[t], n3_sb)):
                nc.scalar.activation(out=dst[:], in_=window[t][:].indirect(offsets[:]), func=ACT.Copy)

        def empty_and_gather(t):
            nc.vector.tensor_copy(out=window[t][:, :V], in_=h_ps[t][:])
            gather_h(t)

        def bend(t, h):
            nc.vector.tensor_tensor(out=diff[t][:], in0=at_n2[t][:], in1=h, op=ALU.subtract)
            nc.scalar.activation(out=bent[t][:], in_=diff[t][:], func=ACT.Tanh)

        def finish(t):
            result = keep.tile([P, V], F32, name=f"result{t}")
            nc.vector.tensor_tensor(out=result[:], in0=bent[t][:], in1=at_n3[t][:], op=ALU.mult)
            nc.sync.dma_start(out=out_rows[t], in_=result[:])

        for u, copy in enumerate((nc.scalar.copy, nc.vector.tensor_copy)):
            cols = slice(u * HALF, (u + 1) * HALF)
            product(h0_ps[u][:], w3_q[0], xh_wd[:, cols], xh_sc[:, cols], True, False)
            product(h0_ps[u][:], w2_q[0], z_wd[:, cols], z_sc[:, cols], False, True)
            copy(out=window[0][:, cols], in_=h0_ps[u][:])
        gather_h(0)

        round_columns(nc.scalar.copy, w2_raw, 1, by_scalar[:, 0])
        round_columns(nc.scalar.copy, w3_raw, 1, by_scalar[:, 1])
        round_columns(nc.scalar.copy, w3_raw, 2, by_scalar[:, 2])
        round_columns(nc.vector.tensor_copy, w2_raw, 2, by_vector[:, 0])
        w2_q[1] = quantise(by_scalar[:, 0], "w2_1")
        w3_q[1] = quantise(by_scalar[:, 1], "w3_1")
        make_h(1)
        w2_q[2] = quantise(by_vector[:, 0], "w2_2")
        w3_q[2] = quantise(by_scalar[:, 2], "w3_2")
        make_h(2)
        empty_and_gather(1)
        round_columns(nc.vector.tensor_copy, w2_raw, 3, by_vector[:, 1])
        round_columns(nc.vector.tensor_copy, w3_raw, 3, by_vector[:, 2])
        bend(0, window[0][:, :V])
        w2_q[3] = quantise(by_vector[:, 1], "w2_3")
        w3_q[3] = quantise(by_vector[:, 2], "w3_3")
        make_h(3)
        empty_and_gather(2)
        bend(1, h_ps[1][:])
        empty_and_gather(3)
        for t in range(2, PACK):
            finish(t - 2)
            bend(t, h_ps[t][:])
        for t in range(PACK - 2, PACK):
            finish(t)
